import numpy as np
import ml_dtypes


def mxq(x, axis, fmt="e4m3"):
    dtype, down = {"e4m3": (ml_dtypes.float8_e4m3fn, 7), "e5m2": (ml_dtypes.float8_e5m2, 14)}[fmt]
    v = np.moveaxis(np.asarray(x, np.float32).astype(ml_dtypes.bfloat16).astype(np.float64), axis, -1)
    blocks = v.reshape(v.shape[:-1] + (-1, 32))
    amax = np.abs(blocks).max(-1, keepdims=True)
    byte = np.maximum(np.where(amax > 0, np.frexp(amax)[1] - 1 + 127, 0) - down, 1)
    scale = np.exp2(byte - 127.0)
    codes = (blocks / scale).astype(np.float32).astype(dtype).astype(np.float64)
    return np.moveaxis((codes * scale).reshape(v.shape), -1, axis)


WIDE = False


def mx_kscale(k):
    if not WIDE:
        return np.ones(k)
    levels = np.array([10, -10, 5, -5, 0])
    if k % 512:
        return np.exp2(np.random.permutation(np.resize(levels, k // 32))).repeat(32)
    a = np.empty((k // 512, 16))
    for p in range(k // 512):
        a[p, :8] = np.random.permutation(np.resize(levels, 8))
        for g in range(8):
            far = levels[np.abs(levels - a[p, g]) >= 10]
            a[p, g + 8] = far[np.random.randint(len(far))]
    return np.exp2(a.ravel()).repeat(32)


def f64(x):
    return np.asarray(x).astype(np.float64)


def striped(idx):
    return np.tile(idx.reshape(-1, 16).T, (8, 1)).astype(np.uint16)


def unstriped(offs):
    return offs[:16].T.reshape(-1).astype(np.int64)


E2M1 = np.array([0.0, 0.5, 1.0, 1.5, 2.0, 3.0, 4.0, 6.0, -0.0, -0.5, -1.0, -1.5, -2.0, -3.0, -4.0, -6.0])


def pack_weight(w, fmt):
    k, n = w.shape
    w = f64(np.asarray(w, np.float32).astype(ml_dtypes.bfloat16)).reshape(k // 32, 32, n)
    amax = np.abs(w).max(1)
    if fmt == "e4m3":
        byte = np.frexp(amax)[1] - 1 + 127 - 7
    else:
        mant, ex = np.frexp(amax / 6.0)
        byte = np.where(mant > 0.5, ex, ex - 1) + 127
    byte = np.clip(np.where(amax > 0, byte, 1), 1, 254)
    scaled = (w * np.exp2(127.0 - byte)[:, None, :]).reshape(k, n).astype(np.float32)
    by_word = np.ascontiguousarray(scaled.reshape(k // 512, 128, 4, n).transpose(0, 1, 3, 2))
    if fmt == "e4m3":
        words = by_word.astype(ml_dtypes.float8_e4m3fn).view(np.uint8)
    else:
        c = by_word.astype(ml_dtypes.float4_e2m1fn).view(np.uint8) & 0xF
        words = (c[..., 0::2] | (c[..., 1::2] << 4)).reshape(k // 512, 128, 2 * n)
    return np.ascontiguousarray(words), np.ascontiguousarray(byte.astype(np.uint8).reshape(k // 512, 16, n))


def unpack_weight(words, scales, fmt):
    g, _, n = scales.shape
    words = np.ascontiguousarray(words).reshape(g, 128, n, -1)
    if fmt == "e4m3":
        vals = words.view(ml_dtypes.float8_e4m3fn).astype(np.float64)
    else:
        nib = np.empty((g, 128, n, 4), np.uint8)
        nib[..., 0::2] = words & 0xF
        nib[..., 1::2] = words >> 4
        vals = E2M1[nib]
    vals = vals * np.repeat(np.exp2(scales.astype(np.float64) - 127.0), 8, axis=1)[..., None]
    return vals.transpose(0, 1, 3, 2).reshape(g * 512, n)


def gelu(v):
    return 0.5 * v * (1.0 + np.tanh(np.sqrt(2.0 / np.pi) * (v + 0.044715 * v**3)))


K, H, T, S, T3, S2, P = 1024, 1024, 4096, 1024, 2048, 512, 512

def setup_inputs():
    n = np.random.standard_normal
    s = mx_kscale(K)[:, None]
    u = mx_kscale(H)[:, None]
    tab_words, tab_scales = pack_weight(n((K, T)) * s, "e4m3")
    tab2_words, tab2_scales = pack_weight(n((H, T3)) / np.sqrt(H) / u, "e4m3")
    w4_words, w4_scales = pack_weight((np.eye(K, H) + 0.6 * n((K, H)) / np.sqrt(K)) / s, "e2m1")
    return {
        "tab_words": tab_words, "tab_scales": tab_scales,
        "offs": striped(np.random.permutation(T)[:S]),
        "tab2_words": tab2_words, "tab2_scales": tab2_scales,
        "offs2": striped(np.random.permutation(T3)[:S2]),
        "pos1": striped(np.random.permutation(S)[:P]),
        "pos2": striped(np.random.permutation(S)[:P]),
        "w1": (n((K, H)) / np.sqrt(K) / s).astype(np.float32),
        "w4_words": w4_words, "w4_scales": w4_scales,
        "gain": (np.exp(0.4 * n(H)) * u[:, 0]).astype(np.float32),
        "elastic": np.exp(0.5 * n((H, P))).astype(np.float32),
        "notes": n((S2, P)).astype(np.float32),
        "weigh": np.exp(0.4 * n(S2)).astype(np.float32),
    }

def reference(tab_words, tab_scales, offs, tab2_words, tab2_scales, offs2, pos1, pos2,
              w1, w4_words, w4_scales, gain, elastic, notes, weigh):
    v = unpack_weight(tab_words, tab_scales, "e4m3")[:, unstriped(offs)]
    v2 = unpack_weight(tab2_words, tab2_scales, "e4m3")[:, unstriped(offs2)]
    w4 = unpack_weight(w4_words, w4_scales, "e2m1")
    wear = mxq(f64(w1), 0, "e4m3").T @ v
    own = w4.T @ v
    h = np.maximum(wear, own) * f64(gain)[:, None]
    x1 = mxq(h[:, unstriped(pos1)], 0, "e4m3")
    x2 = mxq(h[:, unstriped(pos2)] * f64(elastic), 0, "e4m3")
    e = v2.T @ x1 + v2.T @ x2
    return (e + f64(notes)) * f64(weigh)[:, None]

@@ -1,0 +1,318 @@
+from contextlib import ExitStack
+
+import concourse.mybir as mybir
+
+K, H, T, S, T3, S2, PAIRS = 1024, 1024, 4096, 1024, 2048, 512, 512
+FLOPS = 2 * (2 * K * H * S + 2 * H * S2 * PAIRS)
+
+F32 = mybir.dt.float32
+BF16 = mybir.dt.bfloat16
+I32 = mybir.dt.int32
+U32 = mybir.dt.uint32
+U16 = mybir.dt.uint16
+U8 = mybir.dt.uint8
+FP8X4 = mybir.dt.float8_e4m3fn_x4
+FP4X4 = mybir.dt.float4_e2m1fn_x4
+MULT = mybir.AluOpType.mult
+ADD = mybir.AluOpType.add
+MAX = mybir.AluOpType.max
+COPY = mybir.ActivationFunctionType.Copy
+
+P = 128
+PACK = 4
+PASS = P * PACK
+BANK = 512
+HALF = PAIRS // 2
+
+
+def tile_list_wash_recipe_picks_kernel(
+    tc, tab_words, tab_scales, offs, tab2_words, tab2_scales, offs2, pos1, pos2,
+    w1, w4_words, w4_scales, gain, elastic, notes, weigh, out,
+):
+    nc = tc.nc
+    with ExitStack() as ctx:
+        keep = ctx.enter_context(tc.tile_pool(name="keep", bufs=1))
+        ring = ctx.enter_context(tc.tile_pool(name="ring", bufs=2))
+        shared = ctx.enter_context(tc.tile_pool(name="shared", bufs=1))
+        psum = ctx.enter_context(tc.psum_pool(name="psum", bufs=1))
+
+        def held(shape, dtype, name):
+            return keep.tile(shape, dtype, name=name, align_bytes=64)
+
+        def load_list(src, name):
+            lst = keep.tile([P, src.shape[1]], U16, name=name)
+            nc.sync.dma_start(lst[:], src)
+            return lst
+
+        def load_words(src, a, words):
+            nc.sync.dma_start(words[:].bitcast(I32), src[a].rearrange("p n i -> p (n i)").bitcast(I32))
+            return words
+
+        def zeroed(shape, name):
+            plane = held(shape, U8, name)
+            nc.vector.memset(plane[:].bitcast(I32), 0)
+            return plane
+
+        def load_packed_scales(plane, src):
+            for q in range(4):
+                nc.sync.dma_start(
+                    plane[32 * q : 32 * q + 8, :].bitcast(I32), src[:, 4 * q : 4 * q + 4, :].bitcast(I32)
+                )
+
+        def load_w1(a, b, c0, width):
+            if (a, b) == (1, 1):
+                raw = shared.tile([P, PACK, width], F32, name="w1_raw_last", offset=8 * T)
+            else:
+                raw = held([P, PACK, width], F32, "w1_raw_%d_%d_%d" % (a, b, c0))
+            rows = w1[PASS * a : PASS * (a + 1), PASS * b + c0 : PASS * b + c0 + width]
+            nc.sync.dma_start(raw[:], rows.rearrange("(p i) c -> p i c", i=PACK))
+            return raw
+
+        def load_elastic(b):
+            el = held([P, PACK, PAIRS], F32, "elastic_%d" % b)
+            nc.sync.dma_start(el[:], elastic[PASS * b : PASS * (b + 1), :].rearrange("(p t) j -> p t j", t=PACK))
+            return el
+
+        tab_plane = held([P, T], U8, "tab_plane")
+        nc.gpsimd.memset(tab_plane[:, : T // 2].bitcast(I32), 0)
+        nc.vector.memset(tab_plane[:, T // 2 :].bitcast(I32), 0)
+        w4_plane_raw = held([P, 2, H], U8, "w4_plane_raw")
+        nc.vector.memset(w4_plane_raw[:].rearrange("p a c -> p (a c)").bitcast(I32), 0)
+        v_plane_second = zeroed([P, S], "v_plane_second")
+        tab2_plane = zeroed([P, T3], "tab2_plane")
+
+        idx = load_list(offs, "idx")
+        p1 = load_list(pos1, "p1")
+        p2 = load_list(pos2, "p2")
+        idx2 = load_list(offs2, "idx2")
+        gain_sb = held([P, 2, PACK], F32, "gain_sb")
+        nc.sync.dma_start(gain_sb[:], gain.rearrange("(b p t) -> p b t", b=2, t=PACK))
+        weigh_sb = held([P, S2 // P], F32, "weigh_sb")
+        with nc.allow_non_contiguous_dma(reason="one weight to a partition"):
+            nc.sync.dma_start(weigh_sb[:], weigh.rearrange("(u p) -> p u", p=P))
+        w4_raw = held([P, 2, 2 * H], U8, "w4_raw")
+        nc.sync.dma_start(w4_raw[:].bitcast(I32), w4_words.rearrange("a p c -> p a c").bitcast(I32))
+        load_packed_scales(tab_plane, tab_scales)
+        tab = [shared.tile([P, T], U32, name="tab_%d" % a, offset=4 * T * a) for a in range(2)]
+        load_words(tab_words, 0, tab[0])
+        for q in range(4):
+            nc.sync.dma_start(
+                w4_plane_raw[32 * q : 32 * q + 4].bitcast(I32),
+                w4_scales[:, 4 * q : 4 * q + 4, :].rearrange("a r c -> r a c").bitcast(I32),
+            )
+        load_words(tab_words, 1, tab[1])
+        w1_raw = {(0, 0): [load_w1(0, 0, 0, PASS)], (1, 0): [load_w1(1, 0, c0, PASS // 2) for c0 in (0, PASS // 2)]}
+        el = [load_elastic(0)]
+        for a in range(2):
+            w1_raw[a, 1] = [load_w1(a, 1, 0, PASS)]
+        load_packed_scales(tab2_plane, tab2_scales)
+        tab2 = [load_words(tab2_words, b, held([P, T3], U32, "tab2_%d" % b)) for b in range(2)]
+        el.append(load_elastic(1))
+        notes_sb = held([P, S2 // P, PAIRS], F32, "notes_sb")
+        nc.sync.dma_start(notes_sb[:], notes.rearrange("(u p) j -> p u j", p=P))
+
+        v_plane = held([P, S], U8, "v_plane")
+        nc.vector.tensor_copy(v_plane[:], tab_plane[:].indirect(idx[:]))
+        for q in range(4):
+            nc.gpsimd.dma_start(
+                v_plane_second[32 * q : 32 * q + 4, :].bitcast(I32), v_plane[32 * q + 4 : 32 * q + 8, :].bitcast(I32)
+            )
+
+        w4 = held([P, 2, 2, PACK, 2 * P], U8, "w4")
+        nc.vector.tensor_copy(
+            w4[:].bitcast(U16).rearrange("p a b t q -> p (a b) q t"),
+            w4_raw[:].bitcast(U16).rearrange("p a (b q t) -> p (a b) q t", b=2, t=PACK),
+        )
+        w4_plane = held([P, 2, 2, PACK, P], U8, "w4_plane")
+        nc.vector.tensor_copy(
+            w4_plane[:].rearrange("p a b t q -> p (a b) q t"),
+            w4_plane_raw[:].rearrange("p a (b q t) -> p (a b) q t", b=2, t=PACK),
+        )
+
+        v = {}
+        for a in range(2):
+            for n in range(2):
+                v[a, n] = held([P, BANK], U32, "v_%d_%d" % (a, n))
+                nc.vector.tensor_copy(v[a, n][:], tab[a][:].indirect(idx[:, 32 * n : 32 * (n + 1)]))
+
+        w1_codes, w1_plane = {}, {}
+
+        def round_w1(a, b, copies):
+            if b == 0:
+                dealt = ring.tile([P, PACK, P, PACK], BF16, name="w1_dealt", align_bytes=64)
+            else:
+                dealt = ring.tile([P, PACK, P, PACK], BF16, name="w1_dealt_late", tag="own_sb", bufs=4, align_bytes=64)
+            q0 = 0
+            for raw, copy in zip(w1_raw[a, b], copies):
+                q1 = q0 + raw.shape[2] // PACK
+                copy(dealt[:, :, q0:q1, :].rearrange("p t q i -> p q i t"), raw[:].rearrange("p i (q t) -> p q i t", t=PACK))
+                q0 = q1
+            return dealt
+
+        def quantise_w1(a, b, dealt, parts):
+            w1_codes[a, b] = held([P, PASS], U32, "w1_codes_%d_%d" % (a, b))
+            w1_plane[a, b] = held([P, PASS], U8, "w1_plane_%d_%d" % (a, b))
+            flat = dealt[:].rearrange("p t q i -> p (t q i)")
+            width = PASS // parts
+            for c in range(0, PASS, width):
+                nc.vector.quantize_mx(
+                    out=w1_codes[a, b][:, c : c + width].bitcast(FP8X4),
+                    scales=w1_plane[a, b][:, c : c + width],
+                    in_=flat[:, PACK * c : PACK * (c + width)],
+                )
+
+        h = {}
+
+        own_sb = {}
+
+        def shortcut(b, t):
+            own_sb[b, t] = ring.tile([P, S], F32, name="own_sb", bufs=4, align_bytes=64)
+            for n in range(2):
+                cols = slice(BANK * n, BANK * (n + 1))
+                own = psum.tile([P, BANK], F32, name="own_%d" % n)
+                for a in range(2):
+                    nc.tensor.matmul_mx(
+                        out=own[:],
+                        lhsT=w4[:, a, b, t, :].bitcast(FP4X4),
+                        lhsT_scale=w4_plane[:, a, b, t, :],
+                        rhs=v[a, n][:].bitcast(FP8X4),
+                        rhs_scale=(v_plane, v_plane_second)[a][:, cols],
+                        start=(a == 0),
+                        stop=(a == 1),
+                    )
+                nc.scalar.copy(own_sb[b, t][:, cols], own[:])
+
+        def first_stage(b, t):
+            larger = ring.tile([P, S], F32, name="larger")
+            h[b, t] = ring.tile([P, S], F32, name="h", bufs=5)
+            for n in range(2):
+                cols = slice(BANK * n, BANK * (n + 1))
+                wear = psum.tile([P, BANK], F32, name="wear_%d" % n)
+                for a in range(2):
+                    nc.tensor.matmul_mx(
+                        out=wear[:],
+                        lhsT=w1_codes[a, b][:, P * t : P * (t + 1)].bitcast(FP8X4),
+                        lhsT_scale=w1_plane[a, b][:, P * t : P * (t + 1)],
+                        rhs=v[a, n][:].bitcast(FP8X4),
+                        rhs_scale=v_plane[4 * a :, cols],
+                        start=(a == 0),
+                        stop=(a == 1),
+                    )
+                nc.vector.tensor_tensor(larger[:, cols], wear[:], own_sb[b, t][:, cols], MAX)
+                nc.scalar.activation(h[b, t][:, cols], larger[:, cols], COPY, scale=gain_sb[:, b, t : t + 1])
+
+        picked = {}
+        spans = {0: [(0, PAIRS)], 1: [(0, HALF), (HALF, HALF)]}
+        for b in range(2):
+            for c0, width in spans[b]:
+                for x in range(2):
+                    picked[x, b, c0] = shared.tile(
+                        [P, PACK, width], F32, name="picked_%d_%d_%d" % (x, b, c0),
+                        offset=4 * PACK * (2 * (PAIRS * b + c0) + width * x),
+                    )
+
+        def pick(x, b, t, c0, width):
+            lst = (p1, p2)[x][:, c0 // 16 : (c0 + width) // 16]
+            dst = picked[x, b, c0][:, t, :]
+            if x == 0:
+                nc.vector.tensor_copy(dst, h[b, t][:].indirect(lst))
+            else:
+                nc.vector.tensor_tensor(dst, h[b, t][:].indirect(lst), el[b][:, t, c0 : c0 + width], MULT)
+
+        woven = {}
+
+        def weave(x, b, n, copy):
+            c0 = 0 if b == 0 else HALF * n
+            src = picked[x, b, c0][:, :, HALF * n - c0 : HALF * (n + 1) - c0]
+            woven[x, b, n] = ring.tile([P, HALF, PACK], BF16, name="woven", bufs=6, align_bytes=64)
+            copy(
+                woven[x, b, n][:].rearrange("p (c i) t -> p c t i", i=4),
+                src.rearrange("p t (c i) -> p c t i", i=4),
+            )
+
+        e = {}
+        for n in range(2):
+            for k in range(2):
+                e[n, k] = psum.tile([P, 2, HALF], F32, name="e_%d_%d" % (n, k))
+
+        def second_stage(x, b, n, first, last):
+            codes = held([P, HALF], U32, "x_codes_%d_%d_%d" % (x, b, n))
+            plane = held([P, HALF], U8, "x_plane_%d_%d_%d" % (x, b, n))
+            nc.vector.quantize_mx(
+                out=codes[:].bitcast(FP8X4), scales=plane[:], in_=woven[x, b, n][:].rearrange("p j t -> p (j t)")
+            )
+            for u in range(S2 // P):
+                rows = slice(P * u, P * (u + 1))
+                nc.tensor.matmul_mx(
+                    out=e[n, u // 2][:, u % 2, :],
+                    lhsT=v2[b][:, rows].bitcast(FP8X4),
+                    lhsT_scale=v2_plane[4 * b :, rows],
+                    rhs=codes[:].bitcast(FP8X4),
+                    rhs_scale=plane[:],
+                    start=(first and u % 2 == 0),
+                    stop=(last and u % 2 == 1),
+                )
+
+        def finish(n):
+            cols = slice(HALF * n, HALF * (n + 1))
+            for u in range(S2 // P):
+                res = ring.tile([P, HALF], F32, name="res", bufs=4)
+                nc.vector.scalar_tensor_tensor(
+                    res[:], e[n, u // 2][:, u % 2, :], weigh_sb[:, u : u + 1], notes_sb[:, u, cols], MULT, ADD
+                )
+                nc.sync.dma_start(out[P * u : P * (u + 1), cols], res[:])
+
+        for t in range(2):
+            shortcut(0, t)
+        quantise_w1(0, 0, round_w1(0, 0, [nc.vector.tensor_copy]), 1)
+        quantise_w1(1, 0, round_w1(1, 0, [nc.scalar.copy, nc.vector.tensor_copy]), PACK)
+        for t in range(2, PACK):
+            shortcut(0, t)
+
+        first_stage(0, 0)
+        dealt = {}
+        for t in range(PACK):
+            if t + 1 < PACK:
+                first_stage(0, t + 1)
+            if t in (0, 1):
+                dealt[t] = round_w1(t, 1, [nc.scalar.copy])
+            if t == 3:
+                for a in range(2):
+                    quantise_w1(a, 1, dealt[a], 1)
+                first_stage(1, 0)
+            shortcut(1, t)
+            for x in range(2):
+                pick(x, 0, t, 0, PAIRS)
+
+        for n in range(2):
+            for x in range(2):
+                weave(x, 0, n, nc.scalar.copy)
+        v2_plane = shared.tile([P, S2], U8, name="v2_plane", offset=8 * T + 8 * S2, align_bytes=64)
+        nc.vector.tensor_copy(v2_plane[:], tab2_plane[:].indirect(idx2[:]))
+        v2 = []
+        for b in range(2):
+            v2.append(shared.tile([P, S2], U32, name="v2_%d" % b, offset=8 * T + 4 * S2 * b, align_bytes=64))
+            nc.vector.tensor_copy(v2[b][:], tab2[b][:].indirect(idx2[:]))
+
+        for t in range(PACK):
+            if t + 1 < PACK:
+                first_stage(1, t + 1)
+            nc.scalar.activation(notes_sb[:, t, :], notes_sb[:, t, :], COPY, scale=weigh_sb[:, t : t + 1])
+            for x in range(2):
+                pick(x, 1, t, 0, HALF)
+            second_stage(t % 2, 0, t // 2, t % 2 == 0, False)
+
+        for x in range(2):
+            weave(x, 1, 0, nc.scalar.copy)
+        for t in range(PACK):
+            pick(1, 1, t, HALF, HALF)
+        weave(1, 1, 1, nc.scalar.copy)
+        for t in range(PACK):
+            pick(0, 1, t, HALF, HALF)
+        weave(0, 1, 1, nc.scalar.copy)
+        for x in range(2):
+            second_stage(x, 1, 0, False, x == 1)
+        second_stage(1, 1, 1, False, False)
+        second_stage(0, 1, 1, False, True)
+        finish(0)
+        finish(1)

@@ -44,8 +44,10 @@ def tile_list_wash_recipe_picks_kernel(
             nc.sync.dma_start(lst[:], src)
             return lst
 
-        def load_words(src, a, words):
-            nc.sync.dma_start(words[:].bitcast(I32), src[a].rearrange("p n i -> p (n i)").bitcast(I32))
+        def load_words(src, a, words, c0, c1):
+            nc.sync.dma_start(
+                words[:, c0:c1].bitcast(I32), src[a, :, c0:c1, :].rearrange("p n i -> p (n i)").bitcast(I32)
+            )
             return words
 
         def zeroed(shape, name):
@@ -87,36 +89,38 @@ def tile_list_wash_recipe_picks_kernel(
         idx2 = load_list(offs2, "idx2")
         gain_sb = held([P, 2, PACK], F32, "gain_sb")
         nc.sync.dma_start(gain_sb[:], gain.rearrange("(b p t) -> p b t", b=2, t=PACK))
-        weigh_sb = held([P, S2 // P], F32, "weigh_sb")
-        with nc.allow_non_contiguous_dma(reason="one weight to a partition"):
-            nc.sync.dma_start(weigh_sb[:], weigh.rearrange("(u p) -> p u", p=P))
         w4_raw = held([P, 2, 2 * H], U8, "w4_raw")
         nc.sync.dma_start(w4_raw[:].bitcast(I32), w4_words.rearrange("a p c -> p a c").bitcast(I32))
-        load_packed_scales(tab_plane, tab_scales)
         tab = [shared.tile([P, T], U32, name="tab_%d" % a, offset=4 * T * a) for a in range(2)]
-        load_words(tab_words, 0, tab[0])
+        load_words(tab_words, 0, tab[0], 0, T // 4)
+        load_packed_scales(tab_plane, tab_scales)
+        load_words(tab_words, 0, tab[0], T // 4, T)
         for q in range(4):
             nc.sync.dma_start(
                 w4_plane_raw[32 * q : 32 * q + 4].bitcast(I32),
                 w4_scales[:, 4 * q : 4 * q + 4, :].rearrange("a r c -> r a c").bitcast(I32),
             )
-        load_words(tab_words, 1, tab[1])
+        load_words(tab_words, 1, tab[1], 0, T // 2)
+        load_words(tab_words, 1, tab[1], T // 2, T)
+        weigh_sb = held([P, S2 // P], F32, "weigh_sb")
+        with nc.allow_non_contiguous_dma(reason="one weight to a partition"):
+            nc.sync.dma_start(weigh_sb[:], weigh.rearrange("(u p) -> p u", p=P))
+        v_plane = held([P, S], U8, "v_plane")
+        nc.vector.tensor_copy(v_plane[:], tab_plane[:].indirect(idx[:]))
+        for q in range(4):
+            nc.sync.dma_start(
+                v_plane_second[32 * q : 32 * q + 4, :].bitcast(I32), v_plane[32 * q + 4 : 32 * q + 8, :].bitcast(I32)
+            )
         w1_raw = {(0, 0): [load_w1(0, 0, 0, PASS)], (1, 0): [load_w1(1, 0, c0, PASS // 2) for c0 in (0, PASS // 2)]}
         el = [load_elastic(0)]
         for a in range(2):
             w1_raw[a, 1] = [load_w1(a, 1, 0, PASS)]
         load_packed_scales(tab2_plane, tab2_scales)
-        tab2 = [load_words(tab2_words, b, held([P, T3], U32, "tab2_%d" % b)) for b in range(2)]
+        tab2 = [load_words(tab2_words, b, held([P, T3], U32, "tab2_%d" % b), 0, T3) for b in range(2)]
         el.append(load_elastic(1))
         notes_sb = held([P, S2 // P, PAIRS], F32, "notes_sb")
         nc.sync.dma_start(notes_sb[:], notes.rearrange("(u p) j -> p u j", p=P))
 
-        v_plane = held([P, S], U8, "v_plane")
-        nc.vector.tensor_copy(v_plane[:], tab_plane[:].indirect(idx[:]))
-        for q in range(4):
-            nc.gpsimd.dma_start(
-                v_plane_second[32 * q : 32 * q + 4, :].bitcast(I32), v_plane[32 * q + 4 : 32 * q + 8, :].bitcast(I32)
-            )
 
         w4 = held([P, 2, 2, PACK, 2 * P], U8, "w4")
         nc.vector.tensor_copy(

@@ -93,24 +93,23 @@ def tile_list_wash_recipe_picks_kernel(
         nc.sync.dma_start(w4_raw[:].bitcast(I32), w4_words.rearrange("a p c -> p a c").bitcast(I32))
         tab = [shared.tile([P, T], U32, name="tab_%d" % a, offset=4 * T * a) for a in range(2)]
         load_words(tab_words, 0, tab[0], 0, T // 4)
-        load_packed_scales(tab_plane, tab_scales)
-        load_words(tab_words, 0, tab[0], T // 4, T)
-        for q in range(4):
+        nc.sync.dma_start(tab_plane[4:P:8, :].bitcast(I32), tab_scales[1].bitcast(I32))
+        for r in range(4):
             nc.sync.dma_start(
-                w4_plane_raw[32 * q : 32 * q + 4].bitcast(I32),
-                w4_scales[:, 4 * q : 4 * q + 4, :].rearrange("a r c -> r a c").bitcast(I32),
+                tab_plane[r:P:32, :].bitcast(I32), tab_scales[0].rearrange("(q r) c -> r q c", r=4)[r].bitcast(I32)
             )
-        load_words(tab_words, 1, tab[1], 0, T // 2)
-        load_words(tab_words, 1, tab[1], T // 2, T)
-        weigh_sb = held([P, S2 // P], F32, "weigh_sb")
-        with nc.allow_non_contiguous_dma(reason="one weight to a partition"):
-            nc.sync.dma_start(weigh_sb[:], weigh.rearrange("(u p) -> p u", p=P))
+        load_words(tab_words, 0, tab[0], T // 4, T)
+        for r in range(4):
+            nc.sync.dma_start(
+                w4_plane_raw[r:P:32].bitcast(I32),
+                w4_scales.rearrange("a (q r) c -> r q a c", r=4)[r].bitcast(I32),
+            )
+        for c0, c1 in ((0, T // 4), (T // 4, T // 2), (T // 2, T)):
+            load_words(tab_words, 1, tab[1], c0, c1)
         v_plane = held([P, S], U8, "v_plane")
         nc.vector.tensor_copy(v_plane[:], tab_plane[:].indirect(idx[:]))
-        for q in range(4):
-            nc.sync.dma_start(
-                v_plane_second[32 * q : 32 * q + 4, :].bitcast(I32), v_plane[32 * q + 4 : 32 * q + 8, :].bitcast(I32)
-            )
+        for r in range(4):
+            nc.sync.dma_start(v_plane_second[r:P:32, :].bitcast(I32), v_plane[4 + 8 * r : P : 32, :].bitcast(I32))
         w1_raw = {(0, 0): [load_w1(0, 0, 0, PASS)], (1, 0): [load_w1(1, 0, c0, PASS // 2) for c0 in (0, PASS // 2)]}
         el = [load_elastic(0)]
         for a in range(2):
@@ -118,19 +117,22 @@ def tile_list_wash_recipe_picks_kernel(
         load_packed_scales(tab2_plane, tab2_scales)
         tab2 = [load_words(tab2_words, b, held([P, T3], U32, "tab2_%d" % b), 0, T3) for b in range(2)]
         el.append(load_elastic(1))
+        weigh_sb = held([P, S2 // P], F32, "weigh_sb")
+        with nc.allow_non_contiguous_dma(reason="one weight to a partition"):
+            nc.sync.dma_start(weigh_sb[:], weigh.rearrange("(u p) -> p u", p=P))
         notes_sb = held([P, S2 // P, PAIRS], F32, "notes_sb")
         nc.sync.dma_start(notes_sb[:], notes.rearrange("(u p) j -> p u j", p=P))
 
 
         w4 = held([P, 2, 2, PACK, 2 * P], U8, "w4")
         nc.vector.tensor_copy(
-            w4[:].bitcast(U16).rearrange("p a b t q -> p (a b) q t"),
-            w4_raw[:].bitcast(U16).rearrange("p a (b q t) -> p (a b) q t", b=2, t=PACK),
+            w4[:].bitcast(U16).rearrange("p a b t q -> p (a b) t q"),
+            w4_raw[:].bitcast(U16).rearrange("p a (b q t) -> p (a b) t q", b=2, t=PACK),
         )
         w4_plane = held([P, 2, 2, PACK, P], U8, "w4_plane")
         nc.vector.tensor_copy(
-            w4_plane[:].rearrange("p a b t q -> p (a b) q t"),
-            w4_plane_raw[:].rearrange("p a (b q t) -> p (a b) q t", b=2, t=PACK),
+            w4_plane[:].rearrange("p a b t q -> p (a b) t q"),
+            w4_plane_raw[:].rearrange("p a (b q t) -> p (a b) t q", b=2, t=PACK),
         )
 
         v = {}
@@ -198,7 +200,7 @@ def tile_list_wash_recipe_picks_kernel(
                         lhsT=w1_codes[a, b][:, P * t : P * (t + 1)].bitcast(FP8X4),
                         lhsT_scale=w1_plane[a, b][:, P * t : P * (t + 1)],
                         rhs=v[a, n][:].bitcast(FP8X4),
-                        rhs_scale=v_plane[4 * a :, cols],
+                        rhs_scale=(v_plane, v_plane_second)[a][:, cols],
                         start=(a == 0),
                         stop=(a == 1),
                     )

@@ -92,31 +92,36 @@ def tile_list_wash_recipe_picks_kernel(
         w4_raw = held([P, 2, 2 * H], U8, "w4_raw")
         nc.sync.dma_start(w4_raw[:].bitcast(I32), w4_words.rearrange("a p c -> p a c").bitcast(I32))
         tab = [shared.tile([P, T], U32, name="tab_%d" % a, offset=4 * T * a) for a in range(2)]
-        load_words(tab_words, 0, tab[0], 0, T // 4)
+        load_words(tab_words, 0, tab[0], 0, T // 2)
         nc.sync.dma_start(tab_plane[4:P:8, :].bitcast(I32), tab_scales[1].bitcast(I32))
         for r in range(4):
             nc.sync.dma_start(
                 tab_plane[r:P:32, :].bitcast(I32), tab_scales[0].rearrange("(q r) c -> r q c", r=4)[r].bitcast(I32)
             )
-        load_words(tab_words, 0, tab[0], T // 4, T)
+        load_words(tab_words, 0, tab[0], T // 2, T)
         for r in range(4):
             nc.sync.dma_start(
                 w4_plane_raw[r:P:32].bitcast(I32),
                 w4_scales.rearrange("a (q r) c -> r q a c", r=4)[r].bitcast(I32),
             )
-        for c0, c1 in ((0, T // 4), (T // 4, T // 2), (T // 2, T)):
+        w1_raw = {(0, 0): [load_w1(0, 0, 0, PASS)]}
+        for c0, c1 in ((0, T // 4), (T // 4, T // 2)):
             load_words(tab_words, 1, tab[1], c0, c1)
         v_plane = held([P, S], U8, "v_plane")
         nc.vector.tensor_copy(v_plane[:], tab_plane[:].indirect(idx[:]))
         for r in range(4):
             nc.sync.dma_start(v_plane_second[r:P:32, :].bitcast(I32), v_plane[4 + 8 * r : P : 32, :].bitcast(I32))
-        w1_raw = {(0, 0): [load_w1(0, 0, 0, PASS)], (1, 0): [load_w1(1, 0, c0, PASS // 2) for c0 in (0, PASS // 2)]}
+        load_words(tab_words, 1, tab[1], T // 2, T)
+        w1_raw[1, 0] = [load_w1(1, 0, c0, PASS // 2) for c0 in (0, PASS // 2)]
         el = [load_elastic(0)]
         for a in range(2):
             w1_raw[a, 1] = [load_w1(a, 1, 0, PASS)]
-        load_packed_scales(tab2_plane, tab2_scales)
-        tab2 = [load_words(tab2_words, b, held([P, T3], U32, "tab2_%d" % b), 0, T3) for b in range(2)]
         el.append(load_elastic(1))
+        load_packed_scales(tab2_plane, tab2_scales)
+        tab2 = []
+        for b in range(2):
+            tab2.append(shared.tile([P, T3], U32, name="tab2_%d" % b, offset=10 * T + 4 * T3 * b))
+            load_words(tab2_words, b, tab2[b], 0, T3)
         weigh_sb = held([P, S2 // P], F32, "weigh_sb")
         with nc.allow_non_contiguous_dma(reason="one weight to a partition"):
             nc.sync.dma_start(weigh_sb[:], weigh.rearrange("(u p) -> p u", p=P))
@@ -136,10 +141,16 @@ def tile_list_wash_recipe_picks_kernel(
         )
 
         v = {}
-        for a in range(2):
+
+        def look_up_swatches(a):
             for n in range(2):
                 v[a, n] = held([P, BANK], U32, "v_%d_%d" % (a, n))
                 nc.vector.tensor_copy(v[a, n][:], tab[a][:].indirect(idx[:, 32 * n : 32 * (n + 1)]))
+
+        gain_wide = []
+        for b, width in enumerate((PAIRS, HALF)):
+            gain_wide.append(held([P, PACK, width], F32, "gain_wide_%d" % b))
+            nc.scalar.copy(gain_wide[b][:], gain_sb[:, b, :].unsqueeze(2).to_broadcast([P, PACK, width]))
 
         w1_codes, w1_plane = {}, {}
 
@@ -189,11 +200,10 @@ def tile_list_wash_recipe_picks_kernel(
                 nc.scalar.copy(own_sb[b, t][:, cols], own[:])
 
         def first_stage(b, t):
-            larger = ring.tile([P, S], F32, name="larger")
             h[b, t] = ring.tile([P, S], F32, name="h", bufs=5)
             for n in range(2):
                 cols = slice(BANK * n, BANK * (n + 1))
-                wear = psum.tile([P, BANK], F32, name="wear_%d" % n)
+                wear = psum.tile([P, BANK], F32, name="wear", tag="sums", bufs=6)
                 for a in range(2):
                     nc.tensor.matmul_mx(
                         out=wear[:],
@@ -204,42 +214,46 @@ def tile_list_wash_recipe_picks_kernel(
                         start=(a == 0),
                         stop=(a == 1),
                     )
-                nc.vector.tensor_tensor(larger[:, cols], wear[:], own_sb[b, t][:, cols], MAX)
-                nc.scalar.activation(h[b, t][:, cols], larger[:, cols], COPY, scale=gain_sb[:, b, t : t + 1])
+                nc.vector.tensor_tensor(h[b, t][:, cols], wear[:], own_sb[b, t][:, cols], MAX)
 
         picked = {}
         spans = {0: [(0, PAIRS)], 1: [(0, HALF), (HALF, HALF)]}
         for b in range(2):
             for c0, width in spans[b]:
                 for x in range(2):
+                    offset = 10 * T * b + 4 * PACK * (2 * c0 + width * x)
+                    if (x, b, c0) == (0, 1, HALF):
+                        offset = 4 * T
                     picked[x, b, c0] = shared.tile(
-                        [P, PACK, width], F32, name="picked_%d_%d_%d" % (x, b, c0),
-                        offset=4 * PACK * (2 * (PAIRS * b + c0) + width * x),
+                        [P, PACK, width], F32, name="picked_%d_%d_%d" % (x, b, c0), offset=offset
                     )
 
         def pick(x, b, t, c0, width):
             lst = (p1, p2)[x][:, c0 // 16 : (c0 + width) // 16]
             dst = picked[x, b, c0][:, t, :]
-            if x == 0:
-                nc.vector.tensor_copy(dst, h[b, t][:].indirect(lst))
-            else:
-                nc.vector.tensor_tensor(dst, h[b, t][:].indirect(lst), el[b][:, t, c0 : c0 + width], MULT)
+            factor = gain_wide[b][:, t, :] if x == 0 else el[b][:, t, c0 : c0 + width]
+            nc.vector.tensor_tensor(dst, h[b, t][:].indirect(lst), factor, MULT)
+
+        def scale_elastic(b, t):
+            nc.scalar.activation(el[b][:, t, :], el[b][:, t, :], COPY, scale=gain_sb[:, b, t : t + 1])
 
         woven = {}
 
         def weave(x, b, n, copy):
             c0 = 0 if b == 0 else HALF * n
             src = picked[x, b, c0][:, :, HALF * n - c0 : HALF * (n + 1) - c0]
-            woven[x, b, n] = ring.tile([P, HALF, PACK], BF16, name="woven", bufs=6, align_bytes=64)
+            if (b, n) == (1, 0):
+                woven[x, b, n] = shared.tile(
+                    [P, HALF, PACK], BF16, name="woven_%d" % x, offset=4 * T + 2 * HALF * PACK * x, align_bytes=64
+                )
+            else:
+                woven[x, b, n] = ring.tile([P, HALF, PACK], BF16, name="woven", bufs=6, align_bytes=64)
             copy(
                 woven[x, b, n][:].rearrange("p (c i) t -> p c t i", i=4),
                 src.rearrange("p t (c i) -> p c t i", i=4),
             )
 
         e = {}
-        for n in range(2):
-            for k in range(2):
-                e[n, k] = psum.tile([P, 2, HALF], F32, name="e_%d_%d" % (n, k))
 
         def second_stage(x, b, n, first, last):
             codes = held([P, HALF], U32, "x_codes_%d_%d_%d" % (x, b, n))
@@ -249,6 +263,8 @@ def tile_list_wash_recipe_picks_kernel(
             )
             for u in range(S2 // P):
                 rows = slice(P * u, P * (u + 1))
+                if first and u % 2 == 0:
+                    e[n, u // 2] = psum.tile([P, 2, HALF], F32, name="e", tag="sums", bufs=6)
                 nc.tensor.matmul_mx(
                     out=e[n, u // 2][:, u % 2, :],
                     lhsT=v2[b][:, rows].bitcast(FP8X4),
@@ -268,24 +284,28 @@ def tile_list_wash_recipe_picks_kernel(
                 )
                 nc.sync.dma_start(out[P * u : P * (u + 1), cols], res[:])
 
+        look_up_swatches(0)
+        quantise_w1(0, 0, round_w1(0, 0, [nc.scalar.copy]), 1)
+        look_up_swatches(1)
+        dealt_first = round_w1(1, 0, [nc.scalar.copy, nc.vector.tensor_copy])
         for t in range(2):
             shortcut(0, t)
-        quantise_w1(0, 0, round_w1(0, 0, [nc.vector.tensor_copy]), 1)
-        quantise_w1(1, 0, round_w1(1, 0, [nc.scalar.copy, nc.vector.tensor_copy]), PACK)
+        quantise_w1(1, 0, dealt_first, PACK)
+        first_stage(0, 0)
         for t in range(2, PACK):
             shortcut(0, t)
 
-        first_stage(0, 0)
         dealt = {}
         for t in range(PACK):
             if t + 1 < PACK:
                 first_stage(0, t + 1)
-            if t in (0, 1):
-                dealt[t] = round_w1(t, 1, [nc.scalar.copy])
             if t == 3:
                 for a in range(2):
                     quantise_w1(a, 1, dealt[a], 1)
                 first_stage(1, 0)
+            scale_elastic(0, t)
+            if t in (0, 1):
+                dealt[t] = round_w1(t, 1, [nc.scalar.copy])
             shortcut(1, t)
             for x in range(2):
                 pick(x, 0, t, 0, PAIRS)
@@ -303,6 +323,7 @@ def tile_list_wash_recipe_picks_kernel(
         for t in range(PACK):
             if t + 1 < PACK:
                 first_stage(1, t + 1)
+            scale_elastic(1, t)
             nc.scalar.activation(notes_sb[:, t, :], notes_sb[:, t, :], COPY, scale=weigh_sb[:, t : t + 1])
             for x in range(2):
                 pick(x, 1, t, 0, HALF)
@@ -313,11 +334,11 @@ def tile_list_wash_recipe_picks_kernel(
         for t in range(PACK):
             pick(1, 1, t, HALF, HALF)
         weave(1, 1, 1, nc.scalar.copy)
+        for x in range(2):
+            second_stage(x, 1, 0, False, x == 1)
         for t in range(PACK):
             pick(0, 1, t, HALF, HALF)
         weave(0, 1, 1, nc.scalar.copy)
-        for x in range(2):
-            second_stage(x, 1, 0, False, x == 1)
         second_stage(1, 1, 1, False, False)
         second_stage(0, 1, 1, False, True)
         finish(0)

@@ -23,6 +23,18 @@ PACK = 4
 PASS = P * PACK
 BANK = 512
 HALF = PAIRS // 2
+PER_COLUMN = 16
+QUADRANT = 32
+ROW_TILES = S2 // P
+
+SHORTCUT_BUFS = 5
+H_BUFS = 5
+WOVEN_BUFS = 6
+RESULT_BUFS = 4
+
+TAB_AT = (0, 4 * T)
+W1_LAST_AT = 8 * T
+TAB2_AT = W1_LAST_AT + 4 * PACK * PASS
 
 
 def tile_list_wash_recipe_picks_kernel(
@@ -39,31 +51,27 @@ def tile_list_wash_recipe_picks_kernel(
         def held(shape, dtype, name):
             return keep.tile(shape, dtype, name=name, align_bytes=64)
 
-        def load_list(src, name):
-            lst = keep.tile([P, src.shape[1]], U16, name=name)
-            nc.sync.dma_start(lst[:], src)
-            return lst
-
-        def load_words(src, a, words, c0, c1):
-            nc.sync.dma_start(
-                words[:, c0:c1].bitcast(I32), src[a, :, c0:c1, :].rearrange("p n i -> p (n i)").bitcast(I32)
-            )
-            return words
+        def bank(shape, name, number):
+            return psum.tile(shape, F32, name=name, offset=4 * BANK * number)
 
         def zeroed(shape, name):
             plane = held(shape, U8, name)
             nc.vector.memset(plane[:].bitcast(I32), 0)
             return plane
 
-        def load_packed_scales(plane, src):
-            for q in range(4):
-                nc.sync.dma_start(
-                    plane[32 * q : 32 * q + 8, :].bitcast(I32), src[:, 4 * q : 4 * q + 4, :].bitcast(I32)
-                )
+        def load_list(src, name):
+            entries = keep.tile([P, src.shape[1]], U16, name=name)
+            nc.sync.dma_start(entries[:], src)
+            return entries
+
+        def load_words(src, a, words, c0, c1):
+            nc.sync.dma_start(
+                words[:, c0:c1].bitcast(I32), src[a, :, c0:c1, :].rearrange("p n i -> p (n i)").bitcast(I32)
+            )
 
         def load_w1(a, b, c0, width):
             if (a, b) == (1, 1):
-                raw = shared.tile([P, PACK, width], F32, name="w1_raw_last", offset=8 * T)
+                raw = shared.tile([P, PACK, width], F32, name="w1_raw_last", offset=W1_LAST_AT)
             else:
                 raw = held([P, PACK, width], F32, "w1_raw_%d_%d_%d" % (a, b, c0))
             rows = w1[PASS * a : PASS * (a + 1), PASS * b + c0 : PASS * b + c0 + width]
@@ -71,9 +79,10 @@ def tile_list_wash_recipe_picks_kernel(
             return raw
 
         def load_elastic(b):
-            el = held([P, PACK, PAIRS], F32, "elastic_%d" % b)
-            nc.sync.dma_start(el[:], elastic[PASS * b : PASS * (b + 1), :].rearrange("(p t) j -> p t j", t=PACK))
-            return el
+            factors = held([P, PACK, PAIRS], F32, "elastic_%d" % b)
+            rows = elastic[PASS * b : PASS * (b + 1), :]
+            nc.sync.dma_start(factors[:], rows.rearrange("(p t) j -> p t j", t=PACK))
+            return factors
 
         tab_plane = held([P, T], U8, "tab_plane")
         nc.gpsimd.memset(tab_plane[:, : T // 2].bitcast(I32), 0)
@@ -91,17 +100,18 @@ def tile_list_wash_recipe_picks_kernel(
         nc.sync.dma_start(gain_sb[:], gain.rearrange("(b p t) -> p b t", b=2, t=PACK))
         w4_raw = held([P, 2, 2 * H], U8, "w4_raw")
         nc.sync.dma_start(w4_raw[:].bitcast(I32), w4_words.rearrange("a p c -> p a c").bitcast(I32))
-        tab = [shared.tile([P, T], U32, name="tab_%d" % a, offset=4 * T * a) for a in range(2)]
+        tab = [shared.tile([P, T], U32, name="tab_%d" % a, offset=TAB_AT[a]) for a in range(2)]
         load_words(tab_words, 0, tab[0], 0, T // 2)
         nc.sync.dma_start(tab_plane[4:P:8, :].bitcast(I32), tab_scales[1].bitcast(I32))
         for r in range(4):
             nc.sync.dma_start(
-                tab_plane[r:P:32, :].bitcast(I32), tab_scales[0].rearrange("(q r) c -> r q c", r=4)[r].bitcast(I32)
+                tab_plane[r:P:QUADRANT, :].bitcast(I32),
+                tab_scales[0].rearrange("(q r) c -> r q c", r=4)[r].bitcast(I32),
             )
         load_words(tab_words, 0, tab[0], T // 2, T)
         for r in range(4):
             nc.sync.dma_start(
-                w4_plane_raw[r:P:32].bitcast(I32),
+                w4_plane_raw[r:P:QUADRANT].bitcast(I32),
                 w4_scales.rearrange("a (q r) c -> r q a c", r=4)[r].bitcast(I32),
             )
         w1_raw = {(0, 0): [load_w1(0, 0, 0, PASS)]}
@@ -110,24 +120,31 @@ def tile_list_wash_recipe_picks_kernel(
         v_plane = held([P, S], U8, "v_plane")
         nc.vector.tensor_copy(v_plane[:], tab_plane[:].indirect(idx[:]))
         for r in range(4):
-            nc.sync.dma_start(v_plane_second[r:P:32, :].bitcast(I32), v_plane[4 + 8 * r : P : 32, :].bitcast(I32))
+            nc.sync.dma_start(
+                v_plane_second[r:P:QUADRANT, :].bitcast(I32), v_plane[4 + 8 * r : P : QUADRANT, :].bitcast(I32)
+            )
+        v_planes = (v_plane, v_plane_second)
         load_words(tab_words, 1, tab[1], T // 2, T)
         w1_raw[1, 0] = [load_w1(1, 0, c0, PASS // 2) for c0 in (0, PASS // 2)]
-        el = [load_elastic(0)]
+        stretch = [load_elastic(0)]
         for a in range(2):
-            w1_raw[a, 1] = [load_w1(a, 1, 0, PASS)]
-        el.append(load_elastic(1))
-        load_packed_scales(tab2_plane, tab2_scales)
+            whole = load_w1(a, 1, 0, PASS)
+            w1_raw[a, 1] = [whole[:, :, c0 : c0 + PASS // 2] for c0 in (0, PASS // 2)]
+        stretch.append(load_elastic(1))
+        for q in range(4):
+            nc.sync.dma_start(
+                tab2_plane[QUADRANT * q : QUADRANT * q + 8, :].bitcast(I32),
+                tab2_scales[:, 4 * q : 4 * q + 4, :].bitcast(I32),
+            )
         tab2 = []
         for b in range(2):
-            tab2.append(shared.tile([P, T3], U32, name="tab2_%d" % b, offset=10 * T + 4 * T3 * b))
+            tab2.append(shared.tile([P, T3], U32, name="tab2_%d" % b, offset=TAB2_AT + 4 * T3 * b))
             load_words(tab2_words, b, tab2[b], 0, T3)
-        weigh_sb = held([P, S2 // P], F32, "weigh_sb")
+        weigh_sb = held([P, ROW_TILES], F32, "weigh_sb")
         with nc.allow_non_contiguous_dma(reason="one weight to a partition"):
             nc.sync.dma_start(weigh_sb[:], weigh.rearrange("(u p) -> p u", p=P))
-        notes_sb = held([P, S2 // P, PAIRS], F32, "notes_sb")
+        notes_sb = held([P, ROW_TILES, PAIRS], F32, "notes_sb")
         nc.sync.dma_start(notes_sb[:], notes.rearrange("(u p) j -> p u j", p=P))
-
 
         w4 = held([P, 2, 2, PACK, 2 * P], U8, "w4")
         nc.vector.tensor_copy(
@@ -140,29 +157,33 @@ def tile_list_wash_recipe_picks_kernel(
             w4_plane_raw[:].rearrange("p a (b q t) -> p (a b) t q", b=2, t=PACK),
         )
 
-        v = {}
-
-        def look_up_swatches(a):
-            for n in range(2):
-                v[a, n] = held([P, BANK], U32, "v_%d_%d" % (a, n))
-                nc.vector.tensor_copy(v[a, n][:], tab[a][:].indirect(idx[:, 32 * n : 32 * (n + 1)]))
-
         gain_wide = []
         for b, width in enumerate((PAIRS, HALF)):
             gain_wide.append(held([P, PACK, width], F32, "gain_wide_%d" % b))
             nc.scalar.copy(gain_wide[b][:], gain_sb[:, b, :].unsqueeze(2).to_broadcast([P, PACK, width]))
 
-        w1_codes, w1_plane = {}, {}
+        v, w1_codes, w1_plane, own_sb, h, picked, woven, e = {}, {}, {}, {}, {}, {}, {}, {}
+
+        def look_up_swatches(a):
+            for n in range(2):
+                v[a, n] = held([P, BANK], U32, "v_%d_%d" % (a, n))
+                entries = idx[:, BANK // PER_COLUMN * n : BANK // PER_COLUMN * (n + 1)]
+                nc.vector.tensor_copy(v[a, n][:], tab[a][:].indirect(entries))
 
         def round_w1(a, b, copies):
             if b == 0:
                 dealt = ring.tile([P, PACK, P, PACK], BF16, name="w1_dealt", align_bytes=64)
             else:
-                dealt = ring.tile([P, PACK, P, PACK], BF16, name="w1_dealt_late", tag="own_sb", bufs=4, align_bytes=64)
+                dealt = ring.tile(
+                    [P, PACK, P, PACK], BF16, name="w1_dealt_late", tag="own_sb", bufs=SHORTCUT_BUFS, align_bytes=64
+                )
             q0 = 0
             for raw, copy in zip(w1_raw[a, b], copies):
                 q1 = q0 + raw.shape[2] // PACK
-                copy(dealt[:, :, q0:q1, :].rearrange("p t q i -> p q i t"), raw[:].rearrange("p i (q t) -> p q i t", t=PACK))
+                copy(
+                    dealt[:, :, q0:q1, :].rearrange("p t q i -> p q i t"),
+                    raw[:].rearrange("p i (q t) -> p q i t", t=PACK),
+                )
                 q0 = q1
             return dealt
 
@@ -178,82 +199,71 @@ def tile_list_wash_recipe_picks_kernel(
                     in_=flat[:, PACK * c : PACK * (c + width)],
                 )
 
-        h = {}
-
-        own_sb = {}
-
         def shortcut(b, t):
-            own_sb[b, t] = ring.tile([P, S], F32, name="own_sb", bufs=4, align_bytes=64)
+            own_sb[b, t] = ring.tile([P, S], F32, name="own_sb", bufs=SHORTCUT_BUFS, align_bytes=64)
             for n in range(2):
                 cols = slice(BANK * n, BANK * (n + 1))
-                own = psum.tile([P, BANK], F32, name="own_%d" % n)
+                own = bank([P, BANK], "own_%d_%d_%d" % (b, t, n), n if (b, t) == (0, 0) else 2 + n)
                 for a in range(2):
                     nc.tensor.matmul_mx(
                         out=own[:],
                         lhsT=w4[:, a, b, t, :].bitcast(FP4X4),
                         lhsT_scale=w4_plane[:, a, b, t, :],
                         rhs=v[a, n][:].bitcast(FP8X4),
-                        rhs_scale=(v_plane, v_plane_second)[a][:, cols],
+                        rhs_scale=v_planes[a][:, cols],
                         start=(a == 0),
                         stop=(a == 1),
                     )
                 nc.scalar.copy(own_sb[b, t][:, cols], own[:])
 
         def first_stage(b, t):
-            h[b, t] = ring.tile([P, S], F32, name="h", bufs=5)
+            h[b, t] = ring.tile([P, S], F32, name="h", bufs=H_BUFS)
             for n in range(2):
                 cols = slice(BANK * n, BANK * (n + 1))
-                wear = psum.tile([P, BANK], F32, name="wear", tag="sums", bufs=6)
+                wear = bank([P, BANK], "wear_%d_%d_%d" % (b, t, n), 2 + n if (b, t) == (0, 0) else 4 + 2 * (t % 2) + n)
                 for a in range(2):
                     nc.tensor.matmul_mx(
                         out=wear[:],
                         lhsT=w1_codes[a, b][:, P * t : P * (t + 1)].bitcast(FP8X4),
                         lhsT_scale=w1_plane[a, b][:, P * t : P * (t + 1)],
                         rhs=v[a, n][:].bitcast(FP8X4),
-                        rhs_scale=(v_plane, v_plane_second)[a][:, cols],
+                        rhs_scale=v_planes[a][:, cols],
                         start=(a == 0),
                         stop=(a == 1),
                     )
                 nc.vector.tensor_tensor(h[b, t][:, cols], wear[:], own_sb[b, t][:, cols], MAX)
 
-        picked = {}
-        spans = {0: [(0, PAIRS)], 1: [(0, HALF), (HALF, HALF)]}
-        for b in range(2):
-            for c0, width in spans[b]:
+        for b, spans in enumerate(([(0, PAIRS)], [(0, HALF), (HALF, HALF)])):
+            for c0, width in spans:
                 for x in range(2):
-                    offset = 10 * T * b + 4 * PACK * (2 * c0 + width * x)
+                    offset = (TAB_AT[0], TAB2_AT)[b] + 4 * PACK * (2 * c0 + width * x)
                     if (x, b, c0) == (0, 1, HALF):
-                        offset = 4 * T
+                        offset = TAB_AT[1]
                     picked[x, b, c0] = shared.tile(
                         [P, PACK, width], F32, name="picked_%d_%d_%d" % (x, b, c0), offset=offset
                     )
 
+        def scale_stretch(b, t):
+            nc.scalar.activation(stretch[b][:, t, :], stretch[b][:, t, :], COPY, scale=gain_sb[:, b, t : t + 1])
+
         def pick(x, b, t, c0, width):
-            lst = (p1, p2)[x][:, c0 // 16 : (c0 + width) // 16]
-            dst = picked[x, b, c0][:, t, :]
-            factor = gain_wide[b][:, t, :] if x == 0 else el[b][:, t, c0 : c0 + width]
-            nc.vector.tensor_tensor(dst, h[b, t][:].indirect(lst), factor, MULT)
+            entries = (p1, p2)[x][:, c0 // PER_COLUMN : (c0 + width) // PER_COLUMN]
+            factor = gain_wide[b][:, t, :] if x == 0 else stretch[b][:, t, c0 : c0 + width]
+            nc.vector.tensor_tensor(picked[x, b, c0][:, t, :], h[b, t][:].indirect(entries), factor, MULT)
 
-        def scale_elastic(b, t):
-            nc.scalar.activation(el[b][:, t, :], el[b][:, t, :], COPY, scale=gain_sb[:, b, t : t + 1])
-
-        woven = {}
-
-        def weave(x, b, n, copy):
+        def weave(x, b, n):
             c0 = 0 if b == 0 else HALF * n
             src = picked[x, b, c0][:, :, HALF * n - c0 : HALF * (n + 1) - c0]
             if (b, n) == (1, 0):
                 woven[x, b, n] = shared.tile(
-                    [P, HALF, PACK], BF16, name="woven_%d" % x, offset=4 * T + 2 * HALF * PACK * x, align_bytes=64
+                    [P, HALF, PACK], BF16, name="woven_%d" % x, offset=TAB_AT[1] + 2 * HALF * PACK * x, align_bytes=64
                 )
             else:
-                woven[x, b, n] = ring.tile([P, HALF, PACK], BF16, name="woven", bufs=6, align_bytes=64)
-            copy(
+                woven[x, b, n] = ring.tile([P, HALF, PACK], BF16, name="woven", bufs=WOVEN_BUFS, align_bytes=64)
+            nc.scalar.copy(
                 woven[x, b, n][:].rearrange("p (c i) t -> p c t i", i=4),
                 src.rearrange("p t (c i) -> p c t i", i=4),
             )
-
-        e = {}
 
         def second_stage(x, b, n, first, last):
             codes = held([P, HALF], U32, "x_codes_%d_%d_%d" % (x, b, n))
@@ -261,10 +271,10 @@ def tile_list_wash_recipe_picks_kernel(
             nc.vector.quantize_mx(
                 out=codes[:].bitcast(FP8X4), scales=plane[:], in_=woven[x, b, n][:].rearrange("p j t -> p (j t)")
             )
-            for u in range(S2 // P):
+            for u in range(ROW_TILES):
                 rows = slice(P * u, P * (u + 1))
                 if first and u % 2 == 0:
-                    e[n, u // 2] = psum.tile([P, 2, HALF], F32, name="e", tag="sums", bufs=6)
+                    e[n, u // 2] = bank([P, 2, HALF], "e_%d_%d" % (n, u // 2), 2 * n + u // 2)
                 nc.tensor.matmul_mx(
                     out=e[n, u // 2][:, u % 2, :],
                     lhsT=v2[b][:, rows].bitcast(FP8X4),
@@ -277,68 +287,67 @@ def tile_list_wash_recipe_picks_kernel(
 
         def finish(n):
             cols = slice(HALF * n, HALF * (n + 1))
-            for u in range(S2 // P):
-                res = ring.tile([P, HALF], F32, name="res", bufs=4)
+            for u in range(ROW_TILES):
+                result = ring.tile([P, HALF], F32, name="result", bufs=RESULT_BUFS)
                 nc.vector.scalar_tensor_tensor(
-                    res[:], e[n, u // 2][:, u % 2, :], weigh_sb[:, u : u + 1], notes_sb[:, u, cols], MULT, ADD
+                    result[:], e[n, u // 2][:, u % 2, :], weigh_sb[:, u : u + 1], notes_sb[:, u, cols], MULT, ADD
                 )
-                nc.sync.dma_start(out[P * u : P * (u + 1), cols], res[:])
+                nc.sync.dma_start(out[P * u : P * (u + 1), cols], result[:])
 
         look_up_swatches(0)
         quantise_w1(0, 0, round_w1(0, 0, [nc.scalar.copy]), 1)
         look_up_swatches(1)
         dealt_first = round_w1(1, 0, [nc.scalar.copy, nc.vector.tensor_copy])
-        for t in range(2):
-            shortcut(0, t)
+        shortcut(0, 0)
         quantise_w1(1, 0, dealt_first, PACK)
         first_stage(0, 0)
-        for t in range(2, PACK):
+        for t in range(1, PACK):
             shortcut(0, t)
 
-        dealt = {}
+        dealt_late = {}
         for t in range(PACK):
             if t + 1 < PACK:
                 first_stage(0, t + 1)
-            if t == 3:
+            else:
                 for a in range(2):
-                    quantise_w1(a, 1, dealt[a], 1)
+                    quantise_w1(a, 1, dealt_late[a], 1)
                 first_stage(1, 0)
-            scale_elastic(0, t)
-            if t in (0, 1):
-                dealt[t] = round_w1(t, 1, [nc.scalar.copy])
+            scale_stretch(0, t)
+            if t < 2:
+                dealt_late[t] = round_w1(t, 1, [nc.scalar.copy, nc.scalar.copy])
             shortcut(1, t)
             for x in range(2):
                 pick(x, 0, t, 0, PAIRS)
-
         for n in range(2):
             for x in range(2):
-                weave(x, 0, n, nc.scalar.copy)
-        v2_plane = shared.tile([P, S2], U8, name="v2_plane", offset=8 * T + 8 * S2, align_bytes=64)
+                weave(x, 0, n)
+
+        v2_plane = shared.tile([P, S2], U8, name="v2_plane", offset=W1_LAST_AT + 2 * 4 * S2, align_bytes=64)
         nc.vector.tensor_copy(v2_plane[:], tab2_plane[:].indirect(idx2[:]))
         v2 = []
         for b in range(2):
-            v2.append(shared.tile([P, S2], U32, name="v2_%d" % b, offset=8 * T + 4 * S2 * b, align_bytes=64))
+            v2.append(shared.tile([P, S2], U32, name="v2_%d" % b, offset=W1_LAST_AT + 4 * S2 * b, align_bytes=64))
             nc.vector.tensor_copy(v2[b][:], tab2[b][:].indirect(idx2[:]))
 
         for t in range(PACK):
             if t + 1 < PACK:
                 first_stage(1, t + 1)
-            scale_elastic(1, t)
+            scale_stretch(1, t)
             nc.scalar.activation(notes_sb[:, t, :], notes_sb[:, t, :], COPY, scale=weigh_sb[:, t : t + 1])
             for x in range(2):
                 pick(x, 1, t, 0, HALF)
             second_stage(t % 2, 0, t // 2, t % 2 == 0, False)
-
         for x in range(2):
-            weave(x, 1, 0, nc.scalar.copy)
+            weave(x, 1, 0)
+
         for t in range(PACK):
             pick(1, 1, t, HALF, HALF)
-        weave(1, 1, 1, nc.scalar.copy)
+        weave(1, 1, 1)
         for x in range(2):
             second_stage(x, 1, 0, False, x == 1)
         for t in range(PACK):
             pick(0, 1, t, HALF, HALF)
-        weave(0, 1, 1, nc.scalar.copy)
+        weave(0, 1, 1)
         second_stage(1, 1, 1, False, False)
         second_stage(0, 1, 1, False, True)
         finish(0)

from contextlib import ExitStack

import concourse.mybir as mybir

K, H, T, S, T3, S2, PAIRS = 1024, 1024, 4096, 1024, 2048, 512, 512
FLOPS = 2 * (2 * K * H * S + 2 * H * S2 * PAIRS)

F32 = mybir.dt.float32
BF16 = mybir.dt.bfloat16
I32 = mybir.dt.int32
U32 = mybir.dt.uint32
U16 = mybir.dt.uint16
U8 = mybir.dt.uint8
FP8X4 = mybir.dt.float8_e4m3fn_x4
FP4X4 = mybir.dt.float4_e2m1fn_x4
MULT = mybir.AluOpType.mult
ADD = mybir.AluOpType.add
MAX = mybir.AluOpType.max
COPY = mybir.ActivationFunctionType.Copy

P = 128
PACK = 4
PASS = P * PACK
BANK = 512
HALF = PAIRS // 2
PER_COLUMN = 16
QUADRANT = 32
ROW_TILES = S2 // P

SHORTCUT_BUFS = 5
H_BUFS = 5
WOVEN_BUFS = 6
RESULT_BUFS = 4

TAB_AT = (0, 4 * T)
W1_LAST_AT = 8 * T
TAB2_AT = W1_LAST_AT + 4 * PACK * PASS


def tile_list_wash_recipe_picks_kernel(
    tc, tab_words, tab_scales, offs, tab2_words, tab2_scales, offs2, pos1, pos2,
    w1, w4_words, w4_scales, gain, elastic, notes, weigh, out,
):
    nc = tc.nc
    with ExitStack() as ctx:
        keep = ctx.enter_context(tc.tile_pool(name="keep", bufs=1))
        ring = ctx.enter_context(tc.tile_pool(name="ring", bufs=2))
        shared = ctx.enter_context(tc.tile_pool(name="shared", bufs=1))
        psum = ctx.enter_context(tc.psum_pool(name="psum", bufs=1))

        def held(shape, dtype, name):
            return keep.tile(shape, dtype, name=name, align_bytes=64)

        def bank(shape, name, number):
            return psum.tile(shape, F32, name=name, offset=4 * BANK * number)

        def zeroed(shape, name):
            plane = held(shape, U8, name)
            nc.vector.memset(plane[:].bitcast(I32), 0)
            return plane

        def load_list(src, name):
            entries = keep.tile([P, src.shape[1]], U16, name=name)
            nc.sync.dma_start(entries[:], src)
            return entries

        def load_words(src, a, words, c0, c1):
            nc.sync.dma_start(
                words[:, c0:c1].bitcast(I32), src[a, :, c0:c1, :].rearrange("p n i -> p (n i)").bitcast(I32)
            )

        def load_w1(a, b, c0, width):
            if (a, b) == (1, 1):
                raw = shared.tile([P, PACK, width], F32, name="w1_raw_last", offset=W1_LAST_AT)
            else:
                raw = held([P, PACK, width], F32, "w1_raw_%d_%d_%d" % (a, b, c0))
            rows = w1[PASS * a : PASS * (a + 1), PASS * b + c0 : PASS * b + c0 + width]
            nc.sync.dma_start(raw[:], rows.rearrange("(p i) c -> p i c", i=PACK))
            return raw

        def load_elastic(b):
            factors = held([P, PACK, PAIRS], F32, "elastic_%d" % b)
            rows = elastic[PASS * b : PASS * (b + 1), :]
            nc.sync.dma_start(factors[:], rows.rearrange("(p t) j -> p t j", t=PACK))
            return factors

        tab_plane = held([P, T], U8, "tab_plane")
        nc.gpsimd.memset(tab_plane[:, : T // 2].bitcast(I32), 0)
        nc.vector.memset(tab_plane[:, T // 2 :].bitcast(I32), 0)
        w4_plane_raw = held([P, 2, H], U8, "w4_plane_raw")
        nc.vector.memset(w4_plane_raw[:].rearrange("p a c -> p (a c)").bitcast(I32), 0)
        v_plane_second = zeroed([P, S], "v_plane_second")
        tab2_plane = zeroed([P, T3], "tab2_plane")

        idx = load_list(offs, "idx")
        p1 = load_list(pos1, "p1")
        p2 = load_list(pos2, "p2")
        idx2 = load_list(offs2, "idx2")
        gain_sb = held([P, 2, PACK], F32, "gain_sb")
        nc.sync.dma_start(gain_sb[:], gain.rearrange("(b p t) -> p b t", b=2, t=PACK))
        w4_raw = held([P, 2, 2 * H], U8, "w4_raw")
        nc.sync.dma_start(w4_raw[:].bitcast(I32), w4_words.rearrange("a p c -> p a c").bitcast(I32))
        tab = [shared.tile([P, T], U32, name="tab_%d" % a, offset=TAB_AT[a]) for a in range(2)]
        load_words(tab_words, 0, tab[0], 0, T // 2)
        nc.sync.dma_start(tab_plane[4:P:8, :].bitcast(I32), tab_scales[1].bitcast(I32))
        for r in range(4):
            nc.sync.dma_start(
                tab_plane[r:P:QUADRANT, :].bitcast(I32),
                tab_scales[0].rearrange("(q r) c -> r q c", r=4)[r].bitcast(I32),
            )
        load_words(tab_words, 0, tab[0], T // 2, T)
        for r in range(4):
            nc.sync.dma_start(
                w4_plane_raw[r:P:QUADRANT].bitcast(I32),
                w4_scales.rearrange("a (q r) c -> r q a c", r=4)[r].bitcast(I32),
            )
        w1_raw = {(0, 0): [load_w1(0, 0, 0, PASS)]}
        for c0, c1 in ((0, T // 4), (T // 4, T // 2)):
            load_words(tab_words, 1, tab[1], c0, c1)
        v_plane = held([P, S], U8, "v_plane")
        nc.vector.tensor_copy(v_plane[:], tab_plane[:].indirect(idx[:]))
        for r in range(4):
            nc.sync.dma_start(
                v_plane_second[r:P:QUADRANT, :].bitcast(I32), v_plane[4 + 8 * r : P : QUADRANT, :].bitcast(I32)
            )
        v_planes = (v_plane, v_plane_second)
        load_words(tab_words, 1, tab[1], T // 2, T)
        w1_raw[1, 0] = [load_w1(1, 0, c0, PASS // 2) for c0 in (0, PASS // 2)]
        stretch = [load_elastic(0)]
        for a in range(2):
            whole = load_w1(a, 1, 0, PASS)
            w1_raw[a, 1] = [whole[:, :, c0 : c0 + PASS // 2] for c0 in (0, PASS // 2)]
        stretch.append(load_elastic(1))
        for q in range(4):
            nc.sync.dma_start(
                tab2_plane[QUADRANT * q : QUADRANT * q + 8, :].bitcast(I32),
                tab2_scales[:, 4 * q : 4 * q + 4, :].bitcast(I32),
            )
        tab2 = []
        for b in range(2):
            tab2.append(shared.tile([P, T3], U32, name="tab2_%d" % b, offset=TAB2_AT + 4 * T3 * b))
            load_words(tab2_words, b, tab2[b], 0, T3)
        weigh_sb = held([P, ROW_TILES], F32, "weigh_sb")
        with nc.allow_non_contiguous_dma(reason="one weight to a partition"):
            nc.sync.dma_start(weigh_sb[:], weigh.rearrange("(u p) -> p u", p=P))
        notes_sb = held([P, ROW_TILES, PAIRS], F32, "notes_sb")
        nc.sync.dma_start(notes_sb[:], notes.rearrange("(u p) j -> p u j", p=P))

        w4 = held([P, 2, 2, PACK, 2 * P], U8, "w4")
        nc.vector.tensor_copy(
            w4[:].bitcast(U16).rearrange("p a b t q -> p (a b) t q"),
            w4_raw[:].bitcast(U16).rearrange("p a (b q t) -> p (a b) t q", b=2, t=PACK),
        )
        w4_plane = held([P, 2, 2, PACK, P], U8, "w4_plane")
        nc.vector.tensor_copy(
            w4_plane[:].rearrange("p a b t q -> p (a b) t q"),
            w4_plane_raw[:].rearrange("p a (b q t) -> p (a b) t q", b=2, t=PACK),
        )

        gain_wide = []
        for b, width in enumerate((PAIRS, HALF)):
            gain_wide.append(held([P, PACK, width], F32, "gain_wide_%d" % b))
            nc.scalar.copy(gain_wide[b][:], gain_sb[:, b, :].unsqueeze(2).to_broadcast([P, PACK, width]))

        v, w1_codes, w1_plane, own_sb, h, picked, woven, e = {}, {}, {}, {}, {}, {}, {}, {}

        def look_up_swatches(a):
            for n in range(2):
                v[a, n] = held([P, BANK], U32, "v_%d_%d" % (a, n))
                entries = idx[:, BANK // PER_COLUMN * n : BANK // PER_COLUMN * (n + 1)]
                nc.vector.tensor_copy(v[a, n][:], tab[a][:].indirect(entries))

        def round_w1(a, b, copies):
            if b == 0:
                dealt = ring.tile([P, PACK, P, PACK], BF16, name="w1_dealt", align_bytes=64)
            else:
                dealt = ring.tile(
                    [P, PACK, P, PACK], BF16, name="w1_dealt_late", tag="own_sb", bufs=SHORTCUT_BUFS, align_bytes=64
                )
            q0 = 0
            for raw, copy in zip(w1_raw[a, b], copies):
                q1 = q0 + raw.shape[2] // PACK
                copy(
                    dealt[:, :, q0:q1, :].rearrange("p t q i -> p q i t"),
                    raw[:].rearrange("p i (q t) -> p q i t", t=PACK),
                )
                q0 = q1
            return dealt

        def quantise_w1(a, b, dealt, parts):
            w1_codes[a, b] = held([P, PASS], U32, "w1_codes_%d_%d" % (a, b))
            w1_plane[a, b] = held([P, PASS], U8, "w1_plane_%d_%d" % (a, b))
            flat = dealt[:].rearrange("p t q i -> p (t q i)")
            width = PASS // parts
            for c in range(0, PASS, width):
                nc.vector.quantize_mx(
                    out=w1_codes[a, b][:, c : c + width].bitcast(FP8X4),
                    scales=w1_plane[a, b][:, c : c + width],
                    in_=flat[:, PACK * c : PACK * (c + width)],
                )

        def shortcut(b, t):
            own_sb[b, t] = ring.tile([P, S], F32, name="own_sb", bufs=SHORTCUT_BUFS, align_bytes=64)
            for n in range(2):
                cols = slice(BANK * n, BANK * (n + 1))
                own = bank([P, BANK], "own_%d_%d_%d" % (b, t, n), n if (b, t) == (0, 0) else 2 + n)
                for a in range(2):
                    nc.tensor.matmul_mx(
                        out=own[:],
                        lhsT=w4[:, a, b, t, :].bitcast(FP4X4),
                        lhsT_scale=w4_plane[:, a, b, t, :],
                        rhs=v[a, n][:].bitcast(FP8X4),
                        rhs_scale=v_planes[a][:, cols],
                        start=(a == 0),
                        stop=(a == 1),
                    )
                nc.scalar.copy(own_sb[b, t][:, cols], own[:])

        def first_stage(b, t):
            h[b, t] = ring.tile([P, S], F32, name="h", bufs=H_BUFS)
            for n in range(2):
                cols = slice(BANK * n, BANK * (n + 1))
                wear = bank([P, BANK], "wear_%d_%d_%d" % (b, t, n), 2 + n if (b, t) == (0, 0) else 4 + 2 * (t % 2) + n)
                for a in range(2):
                    nc.tensor.matmul_mx(
                        out=wear[:],
                        lhsT=w1_codes[a, b][:, P * t : P * (t + 1)].bitcast(FP8X4),
                        lhsT_scale=w1_plane[a, b][:, P * t : P * (t + 1)],
                        rhs=v[a, n][:].bitcast(FP8X4),
                        rhs_scale=v_planes[a][:, cols],
                        start=(a == 0),
                        stop=(a == 1),
                    )
                nc.vector.tensor_tensor(h[b, t][:, cols], wear[:], own_sb[b, t][:, cols], MAX)

        for b, spans in enumerate(([(0, PAIRS)], [(0, HALF), (HALF, HALF)])):
            for c0, width in spans:
                for x in range(2):
                    offset = (TAB_AT[0], TAB2_AT)[b] + 4 * PACK * (2 * c0 + width * x)
                    if (x, b, c0) == (0, 1, HALF):
                        offset = TAB_AT[1]
                    picked[x, b, c0] = shared.tile(
                        [P, PACK, width], F32, name="picked_%d_%d_%d" % (x, b, c0), offset=offset
                    )

        def scale_stretch(b, t):
            nc.scalar.activation(stretch[b][:, t, :], stretch[b][:, t, :], COPY, scale=gain_sb[:, b, t : t + 1])

        def pick(x, b, t, c0, width):
            entries = (p1, p2)[x][:, c0 // PER_COLUMN : (c0 + width) // PER_COLUMN]
            factor = gain_wide[b][:, t, :] if x == 0 else stretch[b][:, t, c0 : c0 + width]
            nc.vector.tensor_tensor(picked[x, b, c0][:, t, :], h[b, t][:].indirect(entries), factor, MULT)

        def weave(x, b, n):
            c0 = 0 if b == 0 else HALF * n
            src = picked[x, b, c0][:, :, HALF * n - c0 : HALF * (n + 1) - c0]
            if (b, n) == (1, 0):
                woven[x, b, n] = shared.tile(
                    [P, HALF, PACK], BF16, name="woven_%d" % x, offset=TAB_AT[1] + 2 * HALF * PACK * x, align_bytes=64
                )
            else:
                woven[x, b, n] = ring.tile([P, HALF, PACK], BF16, name="woven", bufs=WOVEN_BUFS, align_bytes=64)
            nc.scalar.copy(
                woven[x, b, n][:].rearrange("p (c i) t -> p c t i", i=4),
                src.rearrange("p t (c i) -> p c t i", i=4),
            )

        def second_stage(x, b, n, first, last):
            codes = held([P, HALF], U32, "x_codes_%d_%d_%d" % (x, b, n))
            plane = held([P, HALF], U8, "x_plane_%d_%d_%d" % (x, b, n))
            nc.vector.quantize_mx(
                out=codes[:].bitcast(FP8X4), scales=plane[:], in_=woven[x, b, n][:].rearrange("p j t -> p (j t)")
            )
            for u in range(ROW_TILES):
                rows = slice(P * u, P * (u + 1))
                if first and u % 2 == 0:
                    e[n, u // 2] = bank([P, 2, HALF], "e_%d_%d" % (n, u // 2), 2 * n + u // 2)
                nc.tensor.matmul_mx(
                    out=e[n, u // 2][:, u % 2, :],
                    lhsT=v2[b][:, rows].bitcast(FP8X4),
                    lhsT_scale=v2_plane[4 * b :, rows],
                    rhs=codes[:].bitcast(FP8X4),
                    rhs_scale=plane[:],
                    start=(first and u % 2 == 0),
                    stop=(last and u % 2 == 1),
                )

        def finish(n):
            cols = slice(HALF * n, HALF * (n + 1))
            for u in range(ROW_TILES):
                result = ring.tile([P, HALF], F32, name="result", bufs=RESULT_BUFS)
                nc.vector.scalar_tensor_tensor(
                    result[:], e[n, u // 2][:, u % 2, :], weigh_sb[:, u : u + 1], notes_sb[:, u, cols], MULT, ADD
                )
                nc.sync.dma_start(out[P * u : P * (u + 1), cols], result[:])

        look_up_swatches(0)
        quantise_w1(0, 0, round_w1(0, 0, [nc.scalar.copy]), 1)
        look_up_swatches(1)
        dealt_first = round_w1(1, 0, [nc.scalar.copy, nc.vector.tensor_copy])
        shortcut(0, 0)
        quantise_w1(1, 0, dealt_first, PACK)
        first_stage(0, 0)
        for t in range(1, PACK):
            shortcut(0, t)

        dealt_late = {}
        for t in range(PACK):
            if t + 1 < PACK:
                first_stage(0, t + 1)
            else:
                for a in range(2):
                    quantise_w1(a, 1, dealt_late[a], 1)
                first_stage(1, 0)
            scale_stretch(0, t)
            if t < 2:
                dealt_late[t] = round_w1(t, 1, [nc.scalar.copy, nc.scalar.copy])
            shortcut(1, t)
            for x in range(2):
                pick(x, 0, t, 0, PAIRS)
        for n in range(2):
            for x in range(2):
                weave(x, 0, n)

        v2_plane = shared.tile([P, S2], U8, name="v2_plane", offset=W1_LAST_AT + 2 * 4 * S2, align_bytes=64)
        nc.vector.tensor_copy(v2_plane[:], tab2_plane[:].indirect(idx2[:]))
        v2 = []
        for b in range(2):
            v2.append(shared.tile([P, S2], U32, name="v2_%d" % b, offset=W1_LAST_AT + 4 * S2 * b, align_bytes=64))
            nc.vector.tensor_copy(v2[b][:], tab2[b][:].indirect(idx2[:]))

        for t in range(PACK):
            if t + 1 < PACK:
                first_stage(1, t + 1)
            scale_stretch(1, t)
            nc.scalar.activation(notes_sb[:, t, :], notes_sb[:, t, :], COPY, scale=weigh_sb[:, t : t + 1])
            for x in range(2):
                pick(x, 1, t, 0, HALF)
            second_stage(t % 2, 0, t // 2, t % 2 == 0, False)
        for x in range(2):
            weave(x, 1, 0)

        for t in range(PACK):
            pick(1, 1, t, HALF, HALF)
        weave(1, 1, 1)
        for x in range(2):
            second_stage(x, 1, 0, False, x == 1)
        for t in range(PACK):
            pick(0, 1, t, HALF, HALF)
        weave(0, 1, 1)
        second_stage(1, 1, 1, False, False)
        second_stage(0, 1, 1, False, True)
        finish(0)
        finish(1)
